import numpy as np
import ml_dtypes


def mxq(x, axis, fmt="e4m3"):
    dtype, down = {"e4m3": (ml_dtypes.float8_e4m3fn, 7), "e5m2": (ml_dtypes.float8_e5m2, 14)}[fmt]
    v = np.moveaxis(np.asarray(x, np.float32).astype(ml_dtypes.bfloat16).astype(np.float64), axis, -1)
    blocks = v.reshape(v.shape[:-1] + (-1, 32))
    amax = np.abs(blocks).max(-1, keepdims=True)
    byte = np.maximum(np.where(amax > 0, np.frexp(amax)[1] - 1 + 127, 0) - down, 1)
    scale = np.exp2(byte - 127.0)
    codes = (blocks / scale).astype(np.float32).astype(dtype).astype(np.float64)
    return np.moveaxis((codes * scale).reshape(v.shape), -1, axis)


WIDE = False


def mx_kscale(k):
    if not WIDE:
        return np.ones(k)
    levels = np.array([10, -10, 5, -5, 0])
    if k % 512:
        return np.exp2(np.random.permutation(np.resize(levels, k // 32))).repeat(32)
    a = np.empty((k // 512, 16))
    for p in range(k // 512):
        a[p, :8] = np.random.permutation(np.resize(levels, 8))
        for g in range(8):
            far = levels[np.abs(levels - a[p, g]) >= 10]
            a[p, g + 8] = far[np.random.randint(len(far))]
    return np.exp2(a.ravel()).repeat(32)


def f64(x):
    return np.asarray(x).astype(np.float64)


def striped8(idx):
    return np.asarray(idx).reshape(8, -1, 16).transpose(0, 2, 1).reshape(128, -1).astype(np.uint16)


def unstriped8(offs):
    return offs.reshape(8, 16, -1).transpose(0, 2, 1).reshape(8, -1).astype(np.int64)


def pick8(x, idx, run):
    r = np.arange(len(x))
    return x[r[:, None], idx[r % (8 * run) // run]]


E2M1 = np.array([0.0, 0.5, 1.0, 1.5, 2.0, 3.0, 4.0, 6.0, -0.0, -0.5, -1.0, -1.5, -2.0, -3.0, -4.0, -6.0])


def pack_weight(w, fmt):
    k, n = w.shape
    w = f64(np.asarray(w, np.float32).astype(ml_dtypes.bfloat16)).reshape(k // 32, 32, n)
    amax = np.abs(w).max(1)
    if fmt == "e4m3":
        byte = np.frexp(amax)[1] - 1 + 127 - 7
    else:
        mant, ex = np.frexp(amax / 6.0)
        byte = np.where(mant > 0.5, ex, ex - 1) + 127
    byte = np.clip(np.where(amax > 0, byte, 1), 1, 254)
    scaled = (w * np.exp2(127.0 - byte)[:, None, :]).reshape(k, n).astype(np.float32)
    by_word = np.ascontiguousarray(scaled.reshape(k // 512, 128, 4, n).transpose(0, 1, 3, 2))
    if fmt == "e4m3":
        words = by_word.astype(ml_dtypes.float8_e4m3fn).view(np.uint8)
    else:
        c = by_word.astype(ml_dtypes.float4_e2m1fn).view(np.uint8) & 0xF
        words = (c[..., 0::2] | (c[..., 1::2] << 4)).reshape(k // 512, 128, 2 * n)
    return np.ascontiguousarray(words), np.ascontiguousarray(byte.astype(np.uint8).reshape(k // 512, 16, n))


def unpack_weight(words, scales, fmt):
    g, _, n = scales.shape
    words = np.ascontiguousarray(words).reshape(g, 128, n, -1)
    if fmt == "e4m3":
        vals = words.view(ml_dtypes.float8_e4m3fn).astype(np.float64)
    else:
        nib = np.empty((g, 128, n, 4), np.uint8)
        nib[..., 0::2] = words & 0xF
        nib[..., 1::2] = words >> 4
        vals = E2M1[nib]
    vals = vals * np.repeat(np.exp2(scales.astype(np.float64) - 127.0), 8, axis=1)[..., None]
    return vals.transpose(0, 1, 3, 2).reshape(g * 512, n)


D, T, I, Q = 512, 1024, 512, 128


def setup_inputs():
    n = np.random.standard_normal
    idx = np.stack([np.random.permutation(T)[:I] for _ in range(8)])
    idx2 = np.stack([np.random.permutation(T)[:I] for _ in range(8)])
    idx3 = np.stack([np.random.permutation(T)[:I] for _ in range(8)])
    idx4 = np.stack([np.random.permutation(T)[:I] for _ in range(8)])
    fd = mx_kscale(D)
    cachep = pack_weight(n((D, T)) / fd[:, None], "e2m1")
    tagsp = pack_weight(n((D, T)) / fd[:, None], "e4m3")
    return {
        "query": (n((D, Q)) * 1.0 / np.sqrt(D) * fd[:, None]).astype(np.float32),
        "cache_words": cachep[0],
        "cache_scales": cachep[1],
        "tags_words": tagsp[0],
        "tags_scales": tagsp[1],
        "offs": striped8(idx),
        "offs2": striped8(idx2),
        "offs3": striped8(idx3),
        "offs4": striped8(idx4),
    }


def reference(query, cache_words, cache_scales, tags_words, tags_scales, offs, offs2, offs3, offs4):
    idx = unstriped8(offs)
    idx2 = unstriped8(offs2)
    idx3 = unstriped8(offs3)
    idx4 = unstriped8(offs4)
    cacheu = unpack_weight(cache_words, cache_scales, "e2m1")
    tagsu = unpack_weight(tags_words, tags_scales, "e4m3")
    queryq = mxq(f64(query), 0, "e4m3")
    a = queryq.T @ cacheu
    b = queryq.T @ tagsu
    hi1 = np.maximum(a, b)
    lo1 = np.minimum(a, b)
    f1 = np.zeros((Q, T))
    f1[np.arange(Q)[:, None], idx2[np.arange(Q) % 128 // 16]] = pick8(lo1, idx, 16)
    hh = hi1 - f1
    v = pick8(hh, idx3, 16) + pick8(lo1, idx4, 16)
    f2 = np.zeros((Q, T))
    f2[np.arange(Q)[:, None], idx4[np.arange(Q) % 128 // 16]] = v
    aa = a + f2
    y = pick8(aa, idx3, 16)
    return y

@@ -1,0 +1,145 @@
+from contextlib import ExitStack
+
+import concourse.mybir as mybir
+
+D, T, SLOTS, Q = 512, 1024, 512, 128
+FLOPS = 2 * 2 * D * Q * T
+
+F32 = mybir.dt.float32
+BF16 = mybir.dt.bfloat16
+I32 = mybir.dt.int32
+U32 = mybir.dt.uint32
+U16 = mybir.dt.uint16
+U8 = mybir.dt.uint8
+FP8X4 = mybir.dt.float8_e4m3fn_x4
+FP4X4 = mybir.dt.float4_e2m1fn_x4
+ALU = mybir.AluOpType
+COPY = mybir.ActivationFunctionType.Copy
+
+P = 128
+PACK = 4
+PIECE = 256
+PIECES = T // PIECE
+HALF = SLOTS // 2
+
+
+def tile_attend_twinsort_twin_kernel(tc, query, cache_words, cache_scales, tags_words, tags_scales, offs, offs2, offs3, offs4, out):
+    nc = tc.nc
+    with ExitStack() as ctx:
+        lists = ctx.enter_context(tc.tile_pool(name="lists", bufs=1))
+        sb = ctx.enter_context(tc.tile_pool(name="sb", bufs=1))
+        psum = ctx.enter_context(tc.psum_pool(name="psum", bufs=1))
+
+        W = T // 4
+        q_raw = sb.tile([P, PACK, Q], F32, tag="raw_then_f2b", align_bytes=64)
+        nc.sync.dma_start(out=q_raw[:], in_=query.rearrange("(p j) q -> p j q", j=PACK))
+        c_stage = sb.tile([P, 2, W], I32)
+        c_scale = sb.tile([P, W], I32, align_bytes=64)
+        t_plane = sb.tile([P, 2, W], I32, align_bytes=64)
+        nc.vector.memset(c_scale[:], 0)
+        nc.vector.memset(t_plane[:, 0, :], 0)
+        for h in range(2):
+            rows = cache_scales[0, 8 * h : 8 * h + 8, :].bitcast(I32).rearrange("(g j) c -> j g c", g=2)
+            nc.scalar.dma_start(out=c_stage[64 * h : 64 * h + 4, :, :], in_=rows)
+        for h in range(2):
+            rows = tags_scales[0, 8 * h : 8 * h + 8, :].bitcast(I32).rearrange("(g j) c -> j g c", g=2)
+            nc.scalar.dma_start(out=t_plane[64 * h : 64 * h + 4, :, :], in_=rows)
+        c_words = sb.tile([P, 2 * T], U8, align_bytes=64)
+        nc.sync.dma_start(out=c_words[:].bitcast(I32), in_=cache_words[0].bitcast(I32))
+        t_rows = tags_words[0].rearrange("p n t -> p (n t)")
+        t_words = []
+        for h in range(2):
+            words = sb.tile([P, T // 2], I32, name=f"t_words{h}", align_bytes=64)
+            nc.sync.dma_start(out=words[:], in_=t_rows[:, h * 2 * T : (h + 1) * 2 * T].bitcast(I32))
+            t_words.append(words)
+        idx = []
+        for n, src in enumerate((offs, offs2, offs3, offs4)):
+            held = lists.tile([P, SLOTS // 16], U16, name=f"idx{n}")
+            nc.sync.dma_start(held[:], src)
+            idx.append(held)
+        idx1, idx2, idx3, idx4 = idx
+
+        f1 = [sb.tile([P, T], F32, name="f1_0"), sb.tile([P, T], F32, name="f1_1", tag="f1b_then_lo4b")]
+        for h in range(2):
+            nc.vector.memset(f1[h][:], 0.0)
+        for g in range(4):
+            src = 64 * (g // 2)
+            nc.vector.tensor_copy(out=c_scale[32 * g : 32 * g + 4, :], in_=c_stage[src : src + 4, g % 2, :])
+
+        q_bf = sb.tile([P, Q, PACK], BF16, tag="bf_then_f2a", align_bytes=64)
+        nc.scalar.activation(q_bf[:, 0 : Q // 2, :], q_raw[:, :, 0 : Q // 2].rearrange("p j q -> p q j"), COPY)
+        nc.vector.tensor_copy(out=q_bf[:, Q // 2 :, :], in_=q_raw[:, :, Q // 2 :].rearrange("p j q -> p q j"))
+        q_codes = sb.tile([P, Q], U32, align_bytes=64)
+        q_scale = sb.tile([P, Q], U8, align_bytes=64)
+        nc.vector.quantize_mx(out=q_codes[:].bitcast(FP8X4), scales=q_scale[:], in_=q_bf[:].rearrange("p q j -> p (q j)"))
+
+        for h in range(2):
+            nc.vector.tensor_copy(out=t_plane[64 * h + 32 : 64 * h + 36, 0, :], in_=t_plane[64 * h : 64 * h + 4, 1, :])
+        t_scale = t_plane[:, 0, :].bitcast(U8)
+        f2 = [
+            sb.tile([P, T], F32, name="f2_0", tag="bf_then_f2a", align_bytes=64),
+            sb.tile([P, T], F32, name="f2_1", tag="raw_then_f2b", align_bytes=64),
+        ]
+        for h in range(2):
+            nc.vector.memset(f2[h][:], 0.0)
+
+        a_ps = [psum.tile([P, PIECE], F32, name=f"a_ps{n}") for n in range(PIECES)]
+        b_ps = [psum.tile([P, PIECE], F32, name=f"b_ps{n}") for n in range(PIECES)]
+        a_sb = sb.tile([P, T], F32)
+        lo = sb.tile([P, T], F32)
+        hi = sb.tile([P, T], F32)
+
+        def score_a(n):
+            nc.tensor.matmul_mx(
+                out=a_ps[n][:], lhsT=q_codes[:].bitcast(FP8X4), lhsT_scale=q_scale[:],
+                rhs=c_words[:, 2 * n * PIECE : 2 * (n + 1) * PIECE].bitcast(FP4X4),
+                rhs_scale=c_scale[:].bitcast(U8)[:, n * PIECE : (n + 1) * PIECE], start=True, stop=True)
+            nc.scalar.activation(a_sb[:, n * PIECE : (n + 1) * PIECE], a_ps[n][:], COPY)
+
+        def score_b(n):
+            c0 = (n % 2) * PIECE
+            nc.tensor.matmul_mx(
+                out=b_ps[n][:], lhsT=q_codes[:].bitcast(FP8X4), lhsT_scale=q_scale[:],
+                rhs=t_words[n // 2][:, c0 : c0 + PIECE].bitcast(FP8X4),
+                rhs_scale=t_scale[:, n * PIECE : (n + 1) * PIECE], start=True, stop=True)
+            cols = slice(n * PIECE, (n + 1) * PIECE)
+            nc.vector.tensor_tensor(lo[:, cols], b_ps[n][:], a_sb[:, cols], ALU.min)
+
+        score_a(0)
+        score_a(1)
+        for n in range(PIECES):
+            if n + 2 < PIECES:
+                score_a(n + 2)
+            score_b(n)
+
+        halves = [slice(h * HALF // 16, (h + 1) * HALF // 16) for h in range(2)]
+        picked = [sb.tile([P, HALF], F32, name=f"picked{h}") for h in range(2)]
+        for h in range(2):
+            nc.vector.tensor_copy(picked[h][:], lo[:].indirect(idx1[:, halves[h]]))
+            nc.scalar.activation(f1[h][:].indirect(idx2[:, halves[h]]), picked[h][:], COPY)
+        for n in range(PIECES):
+            cols = slice(n * PIECE, (n + 1) * PIECE)
+            nc.vector.tensor_tensor(hi[:, cols], b_ps[n][:], a_sb[:, cols], ALU.max)
+        lo4 = [sb.tile([P, HALF], F32, name="lo4_0")]
+        nc.vector.tensor_copy(lo4[0][:], lo[:].indirect(idx4[:, halves[0]]))
+        hh_part = sb.tile([P, T], F32)
+        nc.vector.tensor_tensor(hh_part[:], hi[:], f1[0][:], ALU.subtract)
+        hh = sb.tile([P, T], F32)
+        nc.vector.tensor_tensor(hh[:], hh_part[:], f1[1][:], ALU.subtract)
+        v = [sb.tile([P, HALF], F32, name=f"v{h}") for h in range(2)]
+        for h in range(2):
+            if h == 1:
+                lo4.append(sb.tile([P, HALF], F32, name="lo4_1", tag="f1b_then_lo4b"))
+                nc.vector.tensor_copy(lo4[1][:], lo[:].indirect(idx4[:, halves[1]]))
+            nc.vector.tensor_tensor(v[h][:], hh[:].indirect(idx3[:, halves[h]]), lo4[h][:], ALU.add)
+            nc.scalar.activation(f2[h][:].indirect(idx4[:, halves[h]]), v[h][:], COPY)
+        aa_part = sb.tile([P, T], F32)
+        nc.vector.tensor_tensor(aa_part[:], a_sb[:], f2[0][:], ALU.add)
+        aa = sb.tile([P, T], F32)
+        nc.vector.tensor_tensor(aa[:], aa_part[:], f2[1][:], ALU.add)
+        y0 = sb.tile([P, HALF], F32)
+        y1 = sb.tile([P, HALF], F32)
+        nc.vector.tensor_copy(y0[:], aa[:].indirect(idx3[:, halves[0]]))
+        nc.sync.dma_start(out=out[:, 0:HALF], in_=y0[:])
+        nc.scalar.activation(y1[:], aa[:].indirect(idx3[:, halves[1]]), COPY)
+        nc.scalar.dma_start(out=out[:, HALF:SLOTS], in_=y1[:])

@@ -31,21 +31,22 @@ def tile_attend_twinsort_twin_kernel(tc, query, cache_words, cache_scales, tags_
         psum = ctx.enter_context(tc.psum_pool(name="psum", bufs=1))
 
         W = T // 4
-        q_raw = sb.tile([P, PACK, Q], F32, tag="raw_then_f2b", align_bytes=64)
+        q_raw = sb.tile([P, PACK, Q], F32)
         nc.sync.dma_start(out=q_raw[:], in_=query.rearrange("(p j) q -> p j q", j=PACK))
         c_stage = sb.tile([P, 2, W], I32)
+        t_stage = sb.tile([P, 2, W], I32, tag="stage_then_f2a")
         c_scale = sb.tile([P, W], I32, align_bytes=64)
-        t_plane = sb.tile([P, 2, W], I32, align_bytes=64)
+        t_plane = sb.tile([P, W], I32, align_bytes=64)
         nc.vector.memset(c_scale[:], 0)
-        nc.vector.memset(t_plane[:, 0, :], 0)
+        nc.vector.memset(t_plane[:], 0)
         for h in range(2):
             rows = cache_scales[0, 8 * h : 8 * h + 8, :].bitcast(I32).rearrange("(g j) c -> j g c", g=2)
-            nc.scalar.dma_start(out=c_stage[64 * h : 64 * h + 4, :, :], in_=rows)
+            nc.sync.dma_start(out=c_stage[64 * h : 64 * h + 4, :, :], in_=rows)
+        c_words = sb.tile([P, 2 * T], U8, tag="words_f1b_lo4b", align_bytes=64)
+        nc.sync.dma_start(out=c_words[:].bitcast(I32), in_=cache_words[0].bitcast(I32))
         for h in range(2):
             rows = tags_scales[0, 8 * h : 8 * h + 8, :].bitcast(I32).rearrange("(g j) c -> j g c", g=2)
-            nc.scalar.dma_start(out=t_plane[64 * h : 64 * h + 4, :, :], in_=rows)
-        c_words = sb.tile([P, 2 * T], U8, align_bytes=64)
-        nc.sync.dma_start(out=c_words[:].bitcast(I32), in_=cache_words[0].bitcast(I32))
+            nc.sync.dma_start(out=t_stage[64 * h : 64 * h + 4, :, :], in_=rows)
         t_rows = tags_words[0].rearrange("p n t -> p (n t)")
         t_words = []
         for h in range(2):
@@ -59,29 +60,26 @@ def tile_attend_twinsort_twin_kernel(tc, query, cache_words, cache_scales, tags_
             idx.append(held)
         idx1, idx2, idx3, idx4 = idx
 
-        f1 = [sb.tile([P, T], F32, name="f1_0"), sb.tile([P, T], F32, name="f1_1", tag="f1b_then_lo4b")]
-        for h in range(2):
-            nc.vector.memset(f1[h][:], 0.0)
-        for g in range(4):
-            src = 64 * (g // 2)
-            nc.vector.tensor_copy(out=c_scale[32 * g : 32 * g + 4, :], in_=c_stage[src : src + 4, g % 2, :])
+        f1 = [sb.tile([P, T], F32, name="f1_0")]
+        nc.vector.memset(f1[0][:].bitcast(I32), 0)
 
-        q_bf = sb.tile([P, Q, PACK], BF16, tag="bf_then_f2a", align_bytes=64)
+        q_bf = sb.tile([P, Q, PACK], BF16, align_bytes=64)
         nc.scalar.activation(q_bf[:, 0 : Q // 2, :], q_raw[:, :, 0 : Q // 2].rearrange("p j q -> p q j"), COPY)
         nc.vector.tensor_copy(out=q_bf[:, Q // 2 :, :], in_=q_raw[:, :, Q // 2 :].rearrange("p j q -> p q j"))
+        for h in range(2):
+            src = 64 * h
+            nc.scalar.copy(out=c_scale[src : src + 4, :].bitcast(U32), in_=c_stage[src : src + 4, 0, :].bitcast(U32))
+            nc.vector.tensor_copy(out=c_scale[src + 32 : src + 36, :], in_=c_stage[src : src + 4, 1, :])
         q_codes = sb.tile([P, Q], U32, align_bytes=64)
         q_scale = sb.tile([P, Q], U8, align_bytes=64)
         nc.vector.quantize_mx(out=q_codes[:].bitcast(FP8X4), scales=q_scale[:], in_=q_bf[:].rearrange("p q j -> p (q j)"))
 
-        for h in range(2):
-            nc.vector.tensor_copy(out=t_plane[64 * h + 32 : 64 * h + 36, 0, :], in_=t_plane[64 * h : 64 * h + 4, 1, :])
-        t_scale = t_plane[:, 0, :].bitcast(U8)
-        f2 = [
-            sb.tile([P, T], F32, name="f2_0", tag="bf_then_f2a", align_bytes=64),
-            sb.tile([P, T], F32, name="f2_1", tag="raw_then_f2b", align_bytes=64),
-        ]
-        for h in range(2):
-            nc.vector.memset(f2[h][:], 0.0)
+        for g in range(4):
+            src = 64 * (g // 2)
+            nc.vector.tensor_copy(out=t_plane[32 * g : 32 * g + 4, :], in_=t_stage[src : src + 4, g % 2, :])
+        t_scale = t_plane[:].bitcast(U8)
+        f2 = [sb.tile([P, T], F32, name="f2_0", tag="stage_then_f2a")]
+        nc.vector.memset(f2[0][:].bitcast(I32), 0)
 
         a_ps = [psum.tile([P, PIECE], F32, name=f"a_ps{n}") for n in range(PIECES)]
         b_ps = [psum.tile([P, PIECE], F32, name=f"b_ps{n}") for n in range(PIECES)]
@@ -112,11 +110,16 @@ def tile_attend_twinsort_twin_kernel(tc, query, cache_words, cache_scales, tags_
                 score_a(n + 2)
             score_b(n)
 
+        f1.append(sb.tile([P, T], F32, name="f1_1", tag="words_f1b_lo4b", align_bytes=64))
+        nc.gpsimd.memset(f1[1][:], 0.0)
+
         halves = [slice(h * HALF // 16, (h + 1) * HALF // 16) for h in range(2)]
-        picked = [sb.tile([P, HALF], F32, name=f"picked{h}") for h in range(2)]
+        picked = [sb.tile([P, HALF], F32, name="picked0"), sb.tile([P, HALF], F32, name="picked1", tag="picked_then_f2b")]
         for h in range(2):
             nc.vector.tensor_copy(picked[h][:], lo[:].indirect(idx1[:, halves[h]]))
             nc.scalar.activation(f1[h][:].indirect(idx2[:, halves[h]]), picked[h][:], COPY)
+        f2.append(sb.tile([P, T], F32, name="f2_1", tag="picked_then_f2b"))
+        nc.gpsimd.memset(f2[1][:], 0.0)
         for n in range(PIECES):
             cols = slice(n * PIECE, (n + 1) * PIECE)
             nc.vector.tensor_tensor(hi[:, cols], b_ps[n][:], a_sb[:, cols], ALU.max)
@@ -129,7 +132,7 @@ def tile_attend_twinsort_twin_kernel(tc, query, cache_words, cache_scales, tags_
         v = [sb.tile([P, HALF], F32, name=f"v{h}") for h in range(2)]
         for h in range(2):
             if h == 1:
-                lo4.append(sb.tile([P, HALF], F32, name="lo4_1", tag="f1b_then_lo4b"))
+                lo4.append(sb.tile([P, HALF], F32, name="lo4_1", tag="words_f1b_lo4b", align_bytes=64))
                 nc.vector.tensor_copy(lo4[1][:], lo[:].indirect(idx4[:, halves[1]]))
             nc.vector.tensor_tensor(v[h][:], hh[:].indirect(idx3[:, halves[h]]), lo4[h][:], ALU.add)
             nc.scalar.activation(f2[h][:].indirect(idx4[:, halves[h]]), v[h][:], COPY)

from contextlib import ExitStack

import concourse.mybir as mybir

D, T, SLOTS, Q = 512, 1024, 512, 128
FLOPS = 2 * 2 * D * Q * T

F32 = mybir.dt.float32
BF16 = mybir.dt.bfloat16
I32 = mybir.dt.int32
U32 = mybir.dt.uint32
U16 = mybir.dt.uint16
U8 = mybir.dt.uint8
FP8X4 = mybir.dt.float8_e4m3fn_x4
FP4X4 = mybir.dt.float4_e2m1fn_x4
ALU = mybir.AluOpType
COPY = mybir.ActivationFunctionType.Copy

P = 128
PACK = 4
PIECE = 256
PIECES = T // PIECE
HALF = SLOTS // 2


def tile_attend_twinsort_twin_kernel(tc, query, cache_words, cache_scales, tags_words, tags_scales, offs, offs2, offs3, offs4, out):
    nc = tc.nc
    with ExitStack() as ctx:
        lists = ctx.enter_context(tc.tile_pool(name="lists", bufs=1))
        sb = ctx.enter_context(tc.tile_pool(name="sb", bufs=1))
        psum = ctx.enter_context(tc.psum_pool(name="psum", bufs=1))

        W = T // 4
        q_raw = sb.tile([P, PACK, Q], F32)
        nc.sync.dma_start(out=q_raw[:], in_=query.rearrange("(p j) q -> p j q", j=PACK))
        c_stage = sb.tile([P, 2, W], I32)
        t_stage = sb.tile([P, 2, W], I32, tag="stage_then_f2a")
        c_scale = sb.tile([P, W], I32, align_bytes=64)
        t_plane = sb.tile([P, W], I32, align_bytes=64)
        nc.vector.memset(c_scale[:], 0)
        nc.vector.memset(t_plane[:], 0)
        for h in range(2):
            rows = cache_scales[0, 8 * h : 8 * h + 8, :].bitcast(I32).rearrange("(g j) c -> j g c", g=2)
            nc.sync.dma_start(out=c_stage[64 * h : 64 * h + 4, :, :], in_=rows)
        c_words = sb.tile([P, 2 * T], U8, tag="words_f1b_lo4b", align_bytes=64)
        nc.sync.dma_start(out=c_words[:].bitcast(I32), in_=cache_words[0].bitcast(I32))
        for h in range(2):
            rows = tags_scales[0, 8 * h : 8 * h + 8, :].bitcast(I32).rearrange("(g j) c -> j g c", g=2)
            nc.sync.dma_start(out=t_stage[64 * h : 64 * h + 4, :, :], in_=rows)
        t_rows = tags_words[0].rearrange("p n t -> p (n t)")
        t_words = []
        for h in range(2):
            words = sb.tile([P, T // 2], I32, name=f"t_words{h}", align_bytes=64)
            nc.sync.dma_start(out=words[:], in_=t_rows[:, h * 2 * T : (h + 1) * 2 * T].bitcast(I32))
            t_words.append(words)
        idx = []
        for n, src in enumerate((offs, offs2, offs3, offs4)):
            held = lists.tile([P, SLOTS // 16], U16, name=f"idx{n}")
            nc.sync.dma_start(held[:], src)
            idx.append(held)
        idx1, idx2, idx3, idx4 = idx

        f1 = [sb.tile([P, T], F32, name="f1_0")]
        nc.vector.memset(f1[0][:].bitcast(I32), 0)

        q_bf = sb.tile([P, Q, PACK], BF16, align_bytes=64)
        nc.scalar.activation(q_bf[:, 0 : Q // 2, :], q_raw[:, :, 0 : Q // 2].rearrange("p j q -> p q j"), COPY)
        nc.vector.tensor_copy(out=q_bf[:, Q // 2 :, :], in_=q_raw[:, :, Q // 2 :].rearrange("p j q -> p q j"))
        for h in range(2):
            src = 64 * h
            nc.scalar.copy(out=c_scale[src : src + 4, :].bitcast(U32), in_=c_stage[src : src + 4, 0, :].bitcast(U32))
            nc.vector.tensor_copy(out=c_scale[src + 32 : src + 36, :], in_=c_stage[src : src + 4, 1, :])
        q_codes = sb.tile([P, Q], U32, align_bytes=64)
        q_scale = sb.tile([P, Q], U8, align_bytes=64)
        nc.vector.quantize_mx(out=q_codes[:].bitcast(FP8X4), scales=q_scale[:], in_=q_bf[:].rearrange("p q j -> p (q j)"))

        for g in range(4):
            src = 64 * (g // 2)
            nc.vector.tensor_copy(out=t_plane[32 * g : 32 * g + 4, :], in_=t_stage[src : src + 4, g % 2, :])
        t_scale = t_plane[:].bitcast(U8)
        f2 = [sb.tile([P, T], F32, name="f2_0", tag="stage_then_f2a")]
        nc.vector.memset(f2[0][:].bitcast(I32), 0)

        a_ps = [psum.tile([P, PIECE], F32, name=f"a_ps{n}") for n in range(PIECES)]
        b_ps = [psum.tile([P, PIECE], F32, name=f"b_ps{n}") for n in range(PIECES)]
        a_sb = sb.tile([P, T], F32)
        lo = sb.tile([P, T], F32)
        hi = sb.tile([P, T], F32)

        def score_a(n):
            nc.tensor.matmul_mx(
                out=a_ps[n][:], lhsT=q_codes[:].bitcast(FP8X4), lhsT_scale=q_scale[:],
                rhs=c_words[:, 2 * n * PIECE : 2 * (n + 1) * PIECE].bitcast(FP4X4),
                rhs_scale=c_scale[:].bitcast(U8)[:, n * PIECE : (n + 1) * PIECE], start=True, stop=True)
            nc.scalar.activation(a_sb[:, n * PIECE : (n + 1) * PIECE], a_ps[n][:], COPY)

        def score_b(n):
            c0 = (n % 2) * PIECE
            nc.tensor.matmul_mx(
                out=b_ps[n][:], lhsT=q_codes[:].bitcast(FP8X4), lhsT_scale=q_scale[:],
                rhs=t_words[n // 2][:, c0 : c0 + PIECE].bitcast(FP8X4),
                rhs_scale=t_scale[:, n * PIECE : (n + 1) * PIECE], start=True, stop=True)
            cols = slice(n * PIECE, (n + 1) * PIECE)
            nc.vector.tensor_tensor(lo[:, cols], b_ps[n][:], a_sb[:, cols], ALU.min)

        score_a(0)
        score_a(1)
        for n in range(PIECES):
            if n + 2 < PIECES:
                score_a(n + 2)
            score_b(n)

        f1.append(sb.tile([P, T], F32, name="f1_1", tag="words_f1b_lo4b", align_bytes=64))
        nc.gpsimd.memset(f1[1][:], 0.0)

        halves = [slice(h * HALF // 16, (h + 1) * HALF // 16) for h in range(2)]
        picked = [sb.tile([P, HALF], F32, name="picked0"), sb.tile([P, HALF], F32, name="picked1", tag="picked_then_f2b")]
        for h in range(2):
            nc.vector.tensor_copy(picked[h][:], lo[:].indirect(idx1[:, halves[h]]))
            nc.scalar.activation(f1[h][:].indirect(idx2[:, halves[h]]), picked[h][:], COPY)
        f2.append(sb.tile([P, T], F32, name="f2_1", tag="picked_then_f2b"))
        nc.gpsimd.memset(f2[1][:], 0.0)
        for n in range(PIECES):
            cols = slice(n * PIECE, (n + 1) * PIECE)
            nc.vector.tensor_tensor(hi[:, cols], b_ps[n][:], a_sb[:, cols], ALU.max)
        lo4 = [sb.tile([P, HALF], F32, name="lo4_0")]
        nc.vector.tensor_copy(lo4[0][:], lo[:].indirect(idx4[:, halves[0]]))
        hh_part = sb.tile([P, T], F32)
        nc.vector.tensor_tensor(hh_part[:], hi[:], f1[0][:], ALU.subtract)
        hh = sb.tile([P, T], F32)
        nc.vector.tensor_tensor(hh[:], hh_part[:], f1[1][:], ALU.subtract)
        v = [sb.tile([P, HALF], F32, name=f"v{h}") for h in range(2)]
        for h in range(2):
            if h == 1:
                lo4.append(sb.tile([P, HALF], F32, name="lo4_1", tag="words_f1b_lo4b", align_bytes=64))
                nc.vector.tensor_copy(lo4[1][:], lo[:].indirect(idx4[:, halves[1]]))
            nc.vector.tensor_tensor(v[h][:], hh[:].indirect(idx3[:, halves[h]]), lo4[h][:], ALU.add)
            nc.scalar.activation(f2[h][:].indirect(idx4[:, halves[h]]), v[h][:], COPY)
        aa_part = sb.tile([P, T], F32)
        nc.vector.tensor_tensor(aa_part[:], a_sb[:], f2[0][:], ALU.add)
        aa = sb.tile([P, T], F32)
        nc.vector.tensor_tensor(aa[:], aa_part[:], f2[1][:], ALU.add)
        y0 = sb.tile([P, HALF], F32)
        y1 = sb.tile([P, HALF], F32)
        nc.vector.tensor_copy(y0[:], aa[:].indirect(idx3[:, halves[0]]))
        nc.sync.dma_start(out=out[:, 0:HALF], in_=y0[:])
        nc.scalar.activation(y1[:], aa[:].indirect(idx3[:, halves[1]]), COPY)
        nc.scalar.dma_start(out=out[:, HALF:SLOTS], in_=y1[:])
